import numpy as np
import ml_dtypes


def mxq(x, axis, fmt="e4m3"):
    dtype, down = {"e4m3": (ml_dtypes.float8_e4m3fn, 7), "e5m2": (ml_dtypes.float8_e5m2, 14)}[fmt]
    v = np.moveaxis(np.asarray(x, np.float32).astype(ml_dtypes.bfloat16).astype(np.float64), axis, -1)
    blocks = v.reshape(v.shape[:-1] + (-1, 32))
    amax = np.abs(blocks).max(-1, keepdims=True)
    byte = np.maximum(np.where(amax > 0, np.frexp(amax)[1] - 1 + 127, 0) - down, 1)
    scale = np.exp2(byte - 127.0)
    codes = (blocks / scale).astype(np.float32).astype(dtype).astype(np.float64)
    return np.moveaxis((codes * scale).reshape(v.shape), -1, axis)


WIDE = False


def mx_kscale(k):
    if not WIDE:
        return np.ones(k)
    levels = np.array([10, -10, 5, -5, 0])
    if k % 512:
        return np.exp2(np.random.permutation(np.resize(levels, k // 32))).repeat(32)
    a = np.empty((k // 512, 16))
    for p in range(k // 512):
        a[p, :8] = np.random.permutation(np.resize(levels, 8))
        for g in range(8):
            far = levels[np.abs(levels - a[p, g]) >= 10]
            a[p, g + 8] = far[np.random.randint(len(far))]
    return np.exp2(a.ravel()).repeat(32)


def f64(x):
    return np.asarray(x).astype(np.float64)


def striped(idx):
    return np.tile(np.asarray(idx).reshape(-1, 16).T, (8, 1)).astype(np.uint16)


def unstriped(offs):
    return offs[:16].T.reshape(-1).astype(np.int64)


def striped8(idx):
    return np.asarray(idx).reshape(8, -1, 16).transpose(0, 2, 1).reshape(128, -1).astype(np.uint16)


def unstriped8(offs):
    return offs.reshape(8, 16, -1).transpose(0, 2, 1).reshape(8, -1).astype(np.int64)


def pick8(x, idx, run):
    r = np.arange(len(x))
    return x[r[:, None], idx[r % (8 * run) // run]]


E2M1 = np.array([0.0, 0.5, 1.0, 1.5, 2.0, 3.0, 4.0, 6.0, -0.0, -0.5, -1.0, -1.5, -2.0, -3.0, -4.0, -6.0])


def pack_weight(w, fmt):
    k, n = w.shape
    w = f64(np.asarray(w, np.float32).astype(ml_dtypes.bfloat16)).reshape(k // 32, 32, n)
    amax = np.abs(w).max(1)
    if fmt == "e4m3":
        byte = np.frexp(amax)[1] - 1 + 127 - 7
    else:
        mant, ex = np.frexp(amax / 6.0)
        byte = np.where(mant > 0.5, ex, ex - 1) + 127
    byte = np.clip(np.where(amax > 0, byte, 1), 1, 254)
    scaled = (w * np.exp2(127.0 - byte)[:, None, :]).reshape(k, n).astype(np.float32)
    by_word = np.ascontiguousarray(scaled.reshape(k // 512, 128, 4, n).transpose(0, 1, 3, 2))
    if fmt == "e4m3":
        words = by_word.astype(ml_dtypes.float8_e4m3fn).view(np.uint8)
    else:
        c = by_word.astype(ml_dtypes.float4_e2m1fn).view(np.uint8) & 0xF
        words = (c[..., 0::2] | (c[..., 1::2] << 4)).reshape(k // 512, 128, 2 * n)
    return np.ascontiguousarray(words), np.ascontiguousarray(byte.astype(np.uint8).reshape(k // 512, 16, n))


def unpack_weight(words, scales, fmt):
    g, _, n = scales.shape
    words = np.ascontiguousarray(words).reshape(g, 128, n, -1)
    if fmt == "e4m3":
        vals = words.view(ml_dtypes.float8_e4m3fn).astype(np.float64)
    else:
        nib = np.empty((g, 128, n, 4), np.uint8)
        nib[..., 0::2] = words & 0xF
        nib[..., 1::2] = words >> 4
        vals = E2M1[nib]
    vals = vals * np.repeat(np.exp2(scales.astype(np.float64) - 127.0), 8, axis=1)[..., None]
    return vals.transpose(0, 1, 3, 2).reshape(g * 512, n)


K, J, R, T, U, Z, M, O, C, N, S, V = 512, 256, 512, 1024, 1024, 512, 1024, 128, 512, 256, 512, 1024


def setup_inputs():
    n = np.random.standard_normal
    idx = np.random.permutation(T)[:J]
    idx2 = np.stack([np.random.permutation(U)[:J] for _ in range(8)])
    idx3 = np.random.permutation(M)[:J]
    idx4 = np.stack([np.random.permutation(C)[:J] for _ in range(8)])
    idx5 = np.stack([np.random.permutation(C)[:O] for _ in range(8)])
    idx6 = np.stack([np.random.permutation(J)[:O] for _ in range(8)])
    idx7 = np.random.permutation(V)[:O]
    fk = mx_kscale(K)
    fr = mx_kscale(R)
    fz = mx_kscale(Z)
    fs = mx_kscale(S)
    wp = pack_weight(n((K, R)) * 1 / np.sqrt(K) / fk[:, None] * fr, "e2m1")
    xop = pack_weight(n((Z, M)) / fz[:, None], "e2m1")
    w2p = pack_weight(n((Z, R)) * 1 / np.sqrt(Z) * fz[:, None] * fr, "e4m3")
    wbp = pack_weight(n((R, N)) * 1 / np.sqrt(R) / fr[:, None], "e4m3")
    xrp = pack_weight(n((S, V)) / fs[:, None], "e2m1")
    wsp = pack_weight(n((S, N)) * 1 / np.sqrt(S) * fs[:, None], "e4m3")
    return {
        "ta": (np.random.randint(-7, 8, (K, T)).astype(np.float64)).astype(np.float32),
        "tb": (np.random.randint(-7, 8, (K, U)).astype(np.float64)).astype(np.float32),
        "ga": ((np.random.randint(10, 25, (K, 1)) / 64.0) * fk[:, None]).astype(np.float32),
        "gb": ((np.random.randint(4, 13, (K, 1)) / 64.0) * fk[:, None]).astype(np.float32),
        "w_words": wp[0],
        "w_scales": wp[1],
        "xo_words": xop[0],
        "xo_scales": xop[1],
        "w2_words": w2p[0],
        "w2_scales": w2p[1],
        "sa": (np.random.uniform(0.5, 1.6, (R, 1))).astype(np.float32),
        "sb": (np.random.uniform(0.5, 1.6, (R, 1))).astype(np.float32),
        "wb_words": wbp[0],
        "wb_scales": wbp[1],
        "xr_words": xrp[0],
        "xr_scales": xrp[1],
        "ws_words": wsp[0],
        "ws_scales": wsp[1],
        "offs": striped(idx),
        "offs2": striped8(idx2),
        "offs3": striped(idx3),
        "offs4": striped8(idx4),
        "offs5": striped8(idx5),
        "offs6": striped8(idx6),
        "offs7": striped(idx7),
    }


def reference(ta, tb, ga, gb, w_words, w_scales, xo_words, xo_scales, w2_words, w2_scales, sa, sb, wb_words, wb_scales, xr_words, xr_scales, ws_words, ws_scales, offs, offs2, offs3, offs4, offs5, offs6, offs7):
    idx = unstriped(offs)
    idx2 = unstriped8(offs2)
    idx3 = unstriped(offs3)
    idx4 = unstriped8(offs4)
    idx5 = unstriped8(offs5)
    idx6 = unstriped8(offs6)
    idx7 = unstriped(offs7)
    wu = unpack_weight(w_words, w_scales, "e2m1")
    xou = unpack_weight(xo_words, xo_scales, "e2m1")
    w2u = unpack_weight(w2_words, w2_scales, "e4m3")
    wbu = unpack_weight(wb_words, wb_scales, "e4m3")
    xru = unpack_weight(xr_words, xr_scales, "e2m1")
    wsu = unpack_weight(ws_words, ws_scales, "e4m3")
    xc = f64(ta)[:, idx] * f64(ga) + pick8(f64(tb), idx2, 64) * f64(gb)
    xcq = mxq(xc, 0, "e4m3")
    a = wu.T @ xcq
    xoidx3g = xou[:, idx3]
    b = w2u.T @ xoidx3g
    pw = np.zeros((R, C))
    pw[np.arange(R)[:, None], idx4[np.arange(R) % 512 // 64]] = a
    hid = np.maximum(pick8(pw, idx5, 64) * f64(sa), pick8(b, idx6, 64) * f64(sb))
    hidq = mxq(hid, 0, "e4m3")
    xridx7g = xru[:, idx7]
    y = wbu.T @ hidq + wsu.T @ xridx7g
    return y

@@ -1,0 +1,227 @@
+from contextlib import ExitStack
+
+import concourse.mybir as mybir
+
+F32 = mybir.dt.float32
+BF16 = mybir.dt.bfloat16
+I32 = mybir.dt.int32
+U32 = mybir.dt.uint32
+U16 = mybir.dt.uint16
+U8 = mybir.dt.uint8
+FP8X4 = mybir.dt.float8_e4m3fn_x4
+FP4X4 = mybir.dt.float4_e2m1fn_x4
+COPY = mybir.ActivationFunctionType.Copy
+ADD = mybir.AluOpType.add
+MAX = mybir.AluOpType.max
+
+P = 128
+PACK = 4
+SLOTS = 256
+HALF = SLOTS // 2
+HIDDEN = 512
+BOARD = 512
+PLACES = 128
+OUTS = 256
+TABLE = 1024
+
+FLOPS = 335544320
+
+
+def tile_picked_basedetail_plain_two_boardmeet_reminder_plain_kernel(
+    tc, ta, tb, ga, gb, w_words, w_scales, xo_words, xo_scales, w2_words, w2_scales, sa, sb,
+    wb_words, wb_scales, xr_words, xr_scales, ws_words, ws_scales,
+    offs, offs2, offs3, offs4, offs5, offs6, offs7, out,
+):
+    nc = tc.nc
+    with ExitStack() as ctx:
+        keep = ctx.enter_context(tc.tile_pool(name="keep", bufs=1))
+        psum = ctx.enter_context(tc.psum_pool(name="psum", bufs=1))
+
+        def load_list(name, src):
+            tile = keep.tile(list(src.shape), U16, name=name)
+            nc.sync.dma_start(tile[:], src)
+            return tile
+
+        def load_rows(name, src, queue):
+            tile = keep.tile([P, PACK], F32, name=name)
+            queue.dma_start(tile[:], src.rearrange("(p t) o -> p (t o)", t=PACK))
+            return tile
+
+        def load_table(name, src, t):
+            tile = keep.tile([P, TABLE], F32, name=name)
+            nc.sync.dma_start(tile[:], src.rearrange("(p t) c -> p t c", t=PACK)[:, t, :])
+            return tile
+
+        def load_fp4(name, src):
+            tile = keep.tile([P, src.shape[2] // 2], U16, name=name, align_bytes=64)
+            nc.sync.dma_start(tile[:].bitcast(I32), src[0].bitcast(I32))
+            return tile
+
+        def load_fp8(name, src):
+            tile = keep.tile([P, src.shape[2]], I32, name=name, align_bytes=64)
+            nc.sync.dma_start(tile[:], src[0].rearrange("p n t -> p (n t)").bitcast(I32))
+            return tile
+
+        def zero_plane(name, width):
+            tile = keep.tile([P, width], U8, name=name, align_bytes=64)
+            nc.vector.memset(tile[:].bitcast(I32), 0)
+            return tile
+
+        def load_plane(plane, src):
+            rows = src[0].bitcast(I32).rearrange("(q r) n -> r q n", r=4)
+            for r in range(4):
+                nc.sync.dma_start(plane[r:P:32, :].bitcast(I32), rows[r])
+
+        def deal(name, tile, dtype):
+            dealt = keep.tile([P, HIDDEN], dtype, name=name, align_bytes=64)
+            nc.vector.tensor_copy(
+                dealt[:].rearrange("p (t m) -> p t m", t=PACK), tile[:].rearrange("p (m t) -> p t m", t=PACK)
+            )
+            return dealt
+
+        xo_plane = zero_plane("xo_plane", TABLE)
+        w_plane = zero_plane("w_plane", HIDDEN)
+        w2_plane = zero_plane("w2_plane", HIDDEN)
+        xr_plane = zero_plane("xr_plane", TABLE)
+        wb_plane = zero_plane("wb_plane", OUTS)
+        ws_plane = zero_plane("ws_plane", OUTS)
+        boards = []
+        for t in range(PACK):
+            board = keep.tile([P, BOARD], F32, name=f"board{t}")
+            nc.vector.memset(board[:], 0.0)
+            boards.append(board)
+
+        gb_c = load_rows("gb_c", gb, nc.gpsimd)
+        ga_c = load_rows("ga_c", ga, nc.gpsimd)
+        ta_t, tb_t = [None] * PACK, [None] * PACK
+        tb_t[0] = load_table("tb0", tb, 0)
+        l2 = load_list("l2", offs2)
+        ta_t[0] = load_table("ta0", ta, 0)
+        l1 = load_list("l1", offs)
+        load_plane(xo_plane, xo_scales)
+        tb_t[1] = load_table("tb1", tb, 1)
+        xo_w = load_fp4("xo_w", xo_words)
+        l3 = load_list("l3", offs3)
+        ta_t[1] = load_table("ta1", ta, 1)
+        load_plane(w_plane, w_scales)
+        tb_t[2] = load_table("tb2", tb, 2)
+        w_w = load_fp4("w_w", w_words)
+        ta_t[2] = load_table("ta2", ta, 2)
+        load_plane(w2_plane, w2_scales)
+        tb_t[3] = load_table("tb3", tb, 3)
+        ta_t[3] = load_table("ta3", ta, 3)
+        l4 = load_list("l4", offs4)
+        w2_w = load_fp8("w2_w", w2_words)
+        l6 = load_list("l6", offs6)
+        sb_c = load_rows("sb_c", sb, nc.sync)
+        l5 = load_list("l5", offs5)
+        sa_c = load_rows("sa_c", sa, nc.sync)
+        xr_w = load_fp4("xr_w", xr_words)
+        l7 = load_list("l7", offs7)
+        load_plane(xr_plane, xr_scales)
+        ws_w = load_fp8("ws_w", ws_words)
+        load_plane(ws_plane, ws_scales)
+        wb_w = load_fp8("wb_w", wb_words)
+        load_plane(wb_plane, wb_scales)
+
+        xo_gw = keep.tile([P, SLOTS], U16, name="xo_gw", align_bytes=64)
+        xo_gs = keep.tile([P, SLOTS], U8, name="xo_gs", align_bytes=64)
+        nc.vector.tensor_copy(xo_gs[:], xo_plane[:].indirect(l3[:]))
+        nc.vector.tensor_copy(xo_gw[:], xo_w[:].indirect(l3[:]))
+        w_ds = deal("w_ds", w_plane, U8)
+        w_d = deal("w_d", w_w, U16)
+        w2_ds = deal("w2_ds", w2_plane, U8)
+
+        halves = [slice(0, HALF), slice(HALF, SLOTS)]
+        xc = [keep.tile([P, HALF, PACK], BF16, name=f"xc{h}", align_bytes=64) for h in range(2)]
+        xq = keep.tile([P, SLOTS], U32, name="xq", align_bytes=64)
+        xs = keep.tile([P, SLOTS], U8, name="xs", align_bytes=64)
+        for t in range(PACK):
+            detail = keep.tile([P, SLOTS], F32, name=f"detail{t}")
+            base = keep.tile([P, SLOTS], F32, name=f"base{t}")
+            nc.scalar.activation(detail[:], tb_t[t][:].indirect(l2[:]), COPY, scale=gb_c[:, t : t + 1])
+            if t < PACK - 1:
+                nc.scalar.activation(base[:], ta_t[t][:].indirect(l1[:]), COPY, scale=ga_c[:, t : t + 1])
+            for h, js in enumerate(halves):
+                if t == PACK - 1:
+                    nc.scalar.activation(
+                        base[:, js], ta_t[t][:].indirect(l1[:, js.start // 16 : js.stop // 16]), COPY,
+                        scale=ga_c[:, t : t + 1],
+                    )
+                nc.vector.tensor_tensor(xc[h][:, :, t], base[:, js], detail[:, js], ADD)
+                if t == PACK - 1:
+                    nc.vector.quantize_mx(
+                        out=xq[:, js].bitcast(FP8X4), scales=xs[:, js], in_=xc[h][:].rearrange("p j t -> p (j t)")
+                    )
+
+        met_a = keep.tile([P, PACK, PLACES], F32, name="met_a")
+        met_b = keep.tile([P, PACK, PLACES], F32, name="met_b")
+        pieces = [(0, halves[0], "bank4"), (0, halves[1], "bank0")] + [(t, slice(0, SLOTS), f"bank{t}") for t in range(1, PACK)]
+        for i, (t, js, bank) in enumerate(pieces):
+            cols = slice(P * t, P * (t + 1))
+            width = js.stop - js.start
+            acc = psum.tile([P, width], F32, name=f"a_acc{i}", tag=bank)
+            nc.tensor.matmul_mx(
+                out=acc[:], lhsT=w_d[:, cols].bitcast(FP4X4), lhsT_scale=w_ds[:, cols],
+                rhs=xq[:, js].bitcast(FP8X4), rhs_scale=xs[:, js], start=True, stop=True,
+            )
+            a_sb = keep.tile([P, width], F32, name=f"a{i}")
+            nc.scalar.copy(a_sb[:], acc[:])
+            nc.vector.tensor_copy(boards[t][:].indirect(l4[:, js.start // 16 : js.stop // 16]), a_sb[:])
+
+        w2_d = keep.tile([P, HIDDEN], U32, name="w2_d", align_bytes=64)
+        nc.scalar.copy(
+            w2_d[:].rearrange("p (t m) -> p t m", t=PACK), w2_w[:].bitcast(U32).rearrange("p (m t) -> p t m", t=PACK)
+        )
+        b_t = []
+        for t in range(PACK):
+            cols = slice(P * t, P * (t + 1))
+            acc = psum.tile([P, SLOTS], F32, name=f"b_acc{t}", tag=pieces[t][2])
+            nc.tensor.matmul_mx(
+                out=acc[:], lhsT=w2_d[:, cols].bitcast(FP8X4), lhsT_scale=w2_ds[:, cols],
+                rhs=xo_gw[:].bitcast(FP4X4), rhs_scale=xo_gs[:], start=True, stop=True,
+            )
+            b_sb = keep.tile([P, SLOTS], F32, name=f"b{t}")
+            nc.scalar.copy(b_sb[:], acc[:])
+            b_t.append(b_sb)
+        for t in range(PACK):
+            nc.scalar.activation(met_b[:, t, :], b_t[t][:].indirect(l6[:]), COPY, scale=sb_c[:, t : t + 1])
+        for t in range(PACK):
+            nc.scalar.activation(met_a[:, t, :], boards[t][:].indirect(l5[:]), COPY, scale=sa_c[:, t : t + 1])
+
+        xr_gw = keep.tile([P, PLACES], U16, name="xr_gw", align_bytes=64)
+        xr_gs = keep.tile([P, PLACES], U8, name="xr_gs", align_bytes=64)
+        nc.vector.tensor_copy(xr_gw[:], xr_w[:].indirect(l7[:]))
+        nc.vector.tensor_copy(xr_gs[:], xr_plane[:].indirect(l7[:]))
+
+        hid = keep.tile([P, PLACES, PACK], BF16, name="hid", align_bytes=64)
+        for t in range(0, PACK, 2):
+            nc.vector.tensor_tensor(
+                hid[:, :, t : t + 2], met_a[:, t : t + 2, :].rearrange("p t o -> p o t"),
+                met_b[:, t : t + 2, :].rearrange("p t o -> p o t"), MAX,
+            )
+        hq = keep.tile([P, PLACES], U32, name="hq", align_bytes=64)
+        hs = keep.tile([P, PLACES], U8, name="hs", align_bytes=64)
+        nc.vector.quantize_mx(out=hq[:].bitcast(FP8X4), scales=hs[:], in_=hid[:].rearrange("p o t -> p (o t)"))
+
+        accs = []
+        for h in range(2):
+            cols = slice(P * h, P * (h + 1))
+            acc = psum.tile([P, PLACES], F32, name=f"y_acc{h}", tag=f"bank{5 + h}")
+            nc.tensor.matmul_mx(
+                out=acc[:], lhsT=ws_w[:, cols].bitcast(FP8X4), lhsT_scale=ws_plane[:, cols],
+                rhs=xr_gw[:].bitcast(FP4X4), rhs_scale=xr_gs[:], start=True, stop=False,
+            )
+            accs.append(acc)
+        for h in range(2):
+            cols = slice(P * h, P * (h + 1))
+            nc.tensor.matmul_mx(
+                out=accs[h][:], lhsT=wb_w[:, cols].bitcast(FP8X4), lhsT_scale=wb_plane[:, cols],
+                rhs=hq[:].bitcast(FP8X4), rhs_scale=hs[:], start=False, stop=True,
+            )
+        y0 = keep.tile([P, PLACES], F32, name="y0")
+        nc.scalar.copy(y0[:], accs[0][:])
+        nc.scalar.dma_start(out[0:P, :], y0[:])
+        y1 = keep.tile([P, PLACES], F32, name="y1")
+        nc.vector.tensor_copy(y1[:], accs[1][:])
+        nc.sync.dma_start(out[P : 2 * P, :], y1[:])

@@ -67,9 +67,9 @@ def tile_picked_basedetail_plain_two_boardmeet_reminder_plain_kernel(
             nc.vector.memset(tile[:].bitcast(I32), 0)
             return tile
 
-        def load_plane(plane, src):
+        def load_plane(plane, src, which=range(4)):
             rows = src[0].bitcast(I32).rearrange("(q r) n -> r q n", r=4)
-            for r in range(4):
+            for r in which:
                 nc.sync.dma_start(plane[r:P:32, :].bitcast(I32), rows[r])
 
         def deal(name, tile, dtype):
@@ -91,34 +91,38 @@ def tile_picked_basedetail_plain_two_boardmeet_reminder_plain_kernel(
             nc.vector.memset(board[:], 0.0)
             boards.append(board)
 
-        gb_c = load_rows("gb_c", gb, nc.gpsimd)
-        ga_c = load_rows("ga_c", ga, nc.gpsimd)
         ta_t, tb_t = [None] * PACK, [None] * PACK
         tb_t[0] = load_table("tb0", tb, 0)
         l2 = load_list("l2", offs2)
+        gb_c = load_rows("gb_c", gb, nc.sync)
+        load_plane(xo_plane, xo_scales, (0, 1))
         ta_t[0] = load_table("ta0", ta, 0)
-        l1 = load_list("l1", offs)
-        load_plane(xo_plane, xo_scales)
         tb_t[1] = load_table("tb1", tb, 1)
-        xo_w = load_fp4("xo_w", xo_words)
-        l3 = load_list("l3", offs3)
+        load_plane(xo_plane, xo_scales, (2,))
         ta_t[1] = load_table("ta1", ta, 1)
-        load_plane(w_plane, w_scales)
+        load_plane(xo_plane, xo_scales, (3,))
+        l1 = load_list("l1", offs)
+        ga_c = load_rows("ga_c", ga, nc.sync)
+        l3 = load_list("l3", offs3)
         tb_t[2] = load_table("tb2", tb, 2)
-        w_w = load_fp4("w_w", w_words)
+        xo_w = load_fp4("xo_w", xo_words)
+        load_plane(w_plane, w_scales, (0, 1, 2))
         ta_t[2] = load_table("ta2", ta, 2)
-        load_plane(w2_plane, w2_scales)
+        load_plane(w_plane, w_scales, (3,))
+        w_w = load_fp4("w_w", w_words)
+        load_plane(w2_plane, w2_scales, (0, 1))
         tb_t[3] = load_table("tb3", tb, 3)
+        load_plane(w2_plane, w2_scales, (2, 3))
         ta_t[3] = load_table("ta3", ta, 3)
         l4 = load_list("l4", offs4)
         w2_w = load_fp8("w2_w", w2_words)
+        l7 = load_list("l7", offs7)
+        xr_w = load_fp4("xr_w", xr_words)
+        load_plane(xr_plane, xr_scales)
         l6 = load_list("l6", offs6)
         sb_c = load_rows("sb_c", sb, nc.sync)
         l5 = load_list("l5", offs5)
         sa_c = load_rows("sa_c", sa, nc.sync)
-        xr_w = load_fp4("xr_w", xr_words)
-        l7 = load_list("l7", offs7)
-        load_plane(xr_plane, xr_scales)
         ws_w = load_fp8("ws_w", ws_words)
         load_plane(ws_plane, ws_scales)
         wb_w = load_fp8("wb_w", wb_words)

from contextlib import ExitStack

import concourse.mybir as mybir

F32 = mybir.dt.float32
BF16 = mybir.dt.bfloat16
I32 = mybir.dt.int32
U32 = mybir.dt.uint32
U16 = mybir.dt.uint16
U8 = mybir.dt.uint8
FP8X4 = mybir.dt.float8_e4m3fn_x4
FP4X4 = mybir.dt.float4_e2m1fn_x4
COPY = mybir.ActivationFunctionType.Copy
ADD = mybir.AluOpType.add
MAX = mybir.AluOpType.max

P = 128
PACK = 4
SLOTS = 256
HALF = SLOTS // 2
HIDDEN = 512
BOARD = 512
PLACES = 128
OUTS = 256
TABLE = 1024

FLOPS = 335544320


def tile_picked_basedetail_plain_two_boardmeet_reminder_plain_kernel(
    tc, ta, tb, ga, gb, w_words, w_scales, xo_words, xo_scales, w2_words, w2_scales, sa, sb,
    wb_words, wb_scales, xr_words, xr_scales, ws_words, ws_scales,
    offs, offs2, offs3, offs4, offs5, offs6, offs7, out,
):
    nc = tc.nc
    with ExitStack() as ctx:
        keep = ctx.enter_context(tc.tile_pool(name="keep", bufs=1))
        psum = ctx.enter_context(tc.psum_pool(name="psum", bufs=1))

        def load_list(name, src):
            tile = keep.tile(list(src.shape), U16, name=name)
            nc.sync.dma_start(tile[:], src)
            return tile

        def load_rows(name, src, queue):
            tile = keep.tile([P, PACK], F32, name=name)
            queue.dma_start(tile[:], src.rearrange("(p t) o -> p (t o)", t=PACK))
            return tile

        def load_table(name, src, t):
            tile = keep.tile([P, TABLE], F32, name=name)
            nc.sync.dma_start(tile[:], src.rearrange("(p t) c -> p t c", t=PACK)[:, t, :])
            return tile

        def load_fp4(name, src):
            tile = keep.tile([P, src.shape[2] // 2], U16, name=name, align_bytes=64)
            nc.sync.dma_start(tile[:].bitcast(I32), src[0].bitcast(I32))
            return tile

        def load_fp8(name, src):
            tile = keep.tile([P, src.shape[2]], I32, name=name, align_bytes=64)
            nc.sync.dma_start(tile[:], src[0].rearrange("p n t -> p (n t)").bitcast(I32))
            return tile

        def zero_plane(name, width):
            tile = keep.tile([P, width], U8, name=name, align_bytes=64)
            nc.vector.memset(tile[:].bitcast(I32), 0)
            return tile

        def load_plane(plane, src, which=range(4)):
            rows = src[0].bitcast(I32).rearrange("(q r) n -> r q n", r=4)
            for r in which:
                nc.sync.dma_start(plane[r:P:32, :].bitcast(I32), rows[r])

        def deal(name, tile, dtype):
            dealt = keep.tile([P, HIDDEN], dtype, name=name, align_bytes=64)
            nc.vector.tensor_copy(
                dealt[:].rearrange("p (t m) -> p t m", t=PACK), tile[:].rearrange("p (m t) -> p t m", t=PACK)
            )
            return dealt

        xo_plane = zero_plane("xo_plane", TABLE)
        w_plane = zero_plane("w_plane", HIDDEN)
        w2_plane = zero_plane("w2_plane", HIDDEN)
        xr_plane = zero_plane("xr_plane", TABLE)
        wb_plane = zero_plane("wb_plane", OUTS)
        ws_plane = zero_plane("ws_plane", OUTS)
        boards = []
        for t in range(PACK):
            board = keep.tile([P, BOARD], F32, name=f"board{t}")
            nc.vector.memset(board[:], 0.0)
            boards.append(board)

        ta_t, tb_t = [None] * PACK, [None] * PACK
        tb_t[0] = load_table("tb0", tb, 0)
        l2 = load_list("l2", offs2)
        gb_c = load_rows("gb_c", gb, nc.sync)
        load_plane(xo_plane, xo_scales, (0, 1))
        ta_t[0] = load_table("ta0", ta, 0)
        tb_t[1] = load_table("tb1", tb, 1)
        load_plane(xo_plane, xo_scales, (2,))
        ta_t[1] = load_table("ta1", ta, 1)
        load_plane(xo_plane, xo_scales, (3,))
        l1 = load_list("l1", offs)
        ga_c = load_rows("ga_c", ga, nc.sync)
        l3 = load_list("l3", offs3)
        tb_t[2] = load_table("tb2", tb, 2)
        xo_w = load_fp4("xo_w", xo_words)
        load_plane(w_plane, w_scales, (0, 1, 2))
        ta_t[2] = load_table("ta2", ta, 2)
        load_plane(w_plane, w_scales, (3,))
        w_w = load_fp4("w_w", w_words)
        load_plane(w2_plane, w2_scales, (0, 1))
        tb_t[3] = load_table("tb3", tb, 3)
        load_plane(w2_plane, w2_scales, (2, 3))
        ta_t[3] = load_table("ta3", ta, 3)
        l4 = load_list("l4", offs4)
        w2_w = load_fp8("w2_w", w2_words)
        l7 = load_list("l7", offs7)
        xr_w = load_fp4("xr_w", xr_words)
        load_plane(xr_plane, xr_scales)
        l6 = load_list("l6", offs6)
        sb_c = load_rows("sb_c", sb, nc.sync)
        l5 = load_list("l5", offs5)
        sa_c = load_rows("sa_c", sa, nc.sync)
        ws_w = load_fp8("ws_w", ws_words)
        load_plane(ws_plane, ws_scales)
        wb_w = load_fp8("wb_w", wb_words)
        load_plane(wb_plane, wb_scales)

        xo_gw = keep.tile([P, SLOTS], U16, name="xo_gw", align_bytes=64)
        xo_gs = keep.tile([P, SLOTS], U8, name="xo_gs", align_bytes=64)
        nc.vector.tensor_copy(xo_gs[:], xo_plane[:].indirect(l3[:]))
        nc.vector.tensor_copy(xo_gw[:], xo_w[:].indirect(l3[:]))
        w_ds = deal("w_ds", w_plane, U8)
        w_d = deal("w_d", w_w, U16)
        w2_ds = deal("w2_ds", w2_plane, U8)

        halves = [slice(0, HALF), slice(HALF, SLOTS)]
        xc = [keep.tile([P, HALF, PACK], BF16, name=f"xc{h}", align_bytes=64) for h in range(2)]
        xq = keep.tile([P, SLOTS], U32, name="xq", align_bytes=64)
        xs = keep.tile([P, SLOTS], U8, name="xs", align_bytes=64)
        for t in range(PACK):
            detail = keep.tile([P, SLOTS], F32, name=f"detail{t}")
            base = keep.tile([P, SLOTS], F32, name=f"base{t}")
            nc.scalar.activation(detail[:], tb_t[t][:].indirect(l2[:]), COPY, scale=gb_c[:, t : t + 1])
            if t < PACK - 1:
                nc.scalar.activation(base[:], ta_t[t][:].indirect(l1[:]), COPY, scale=ga_c[:, t : t + 1])
            for h, js in enumerate(halves):
                if t == PACK - 1:
                    nc.scalar.activation(
                        base[:, js], ta_t[t][:].indirect(l1[:, js.start // 16 : js.stop // 16]), COPY,
                        scale=ga_c[:, t : t + 1],
                    )
                nc.vector.tensor_tensor(xc[h][:, :, t], base[:, js], detail[:, js], ADD)
                if t == PACK - 1:
                    nc.vector.quantize_mx(
                        out=xq[:, js].bitcast(FP8X4), scales=xs[:, js], in_=xc[h][:].rearrange("p j t -> p (j t)")
                    )

        met_a = keep.tile([P, PACK, PLACES], F32, name="met_a")
        met_b = keep.tile([P, PACK, PLACES], F32, name="met_b")
        pieces = [(0, halves[0], "bank4"), (0, halves[1], "bank0")] + [(t, slice(0, SLOTS), f"bank{t}") for t in range(1, PACK)]
        for i, (t, js, bank) in enumerate(pieces):
            cols = slice(P * t, P * (t + 1))
            width = js.stop - js.start
            acc = psum.tile([P, width], F32, name=f"a_acc{i}", tag=bank)
            nc.tensor.matmul_mx(
                out=acc[:], lhsT=w_d[:, cols].bitcast(FP4X4), lhsT_scale=w_ds[:, cols],
                rhs=xq[:, js].bitcast(FP8X4), rhs_scale=xs[:, js], start=True, stop=True,
            )
            a_sb = keep.tile([P, width], F32, name=f"a{i}")
            nc.scalar.copy(a_sb[:], acc[:])
            nc.vector.tensor_copy(boards[t][:].indirect(l4[:, js.start // 16 : js.stop // 16]), a_sb[:])

        w2_d = keep.tile([P, HIDDEN], U32, name="w2_d", align_bytes=64)
        nc.scalar.copy(
            w2_d[:].rearrange("p (t m) -> p t m", t=PACK), w2_w[:].bitcast(U32).rearrange("p (m t) -> p t m", t=PACK)
        )
        b_t = []
        for t in range(PACK):
            cols = slice(P * t, P * (t + 1))
            acc = psum.tile([P, SLOTS], F32, name=f"b_acc{t}", tag=pieces[t][2])
            nc.tensor.matmul_mx(
                out=acc[:], lhsT=w2_d[:, cols].bitcast(FP8X4), lhsT_scale=w2_ds[:, cols],
                rhs=xo_gw[:].bitcast(FP4X4), rhs_scale=xo_gs[:], start=True, stop=True,
            )
            b_sb = keep.tile([P, SLOTS], F32, name=f"b{t}")
            nc.scalar.copy(b_sb[:], acc[:])
            b_t.append(b_sb)
        for t in range(PACK):
            nc.scalar.activation(met_b[:, t, :], b_t[t][:].indirect(l6[:]), COPY, scale=sb_c[:, t : t + 1])
        for t in range(PACK):
            nc.scalar.activation(met_a[:, t, :], boards[t][:].indirect(l5[:]), COPY, scale=sa_c[:, t : t + 1])

        xr_gw = keep.tile([P, PLACES], U16, name="xr_gw", align_bytes=64)
        xr_gs = keep.tile([P, PLACES], U8, name="xr_gs", align_bytes=64)
        nc.vector.tensor_copy(xr_gw[:], xr_w[:].indirect(l7[:]))
        nc.vector.tensor_copy(xr_gs[:], xr_plane[:].indirect(l7[:]))

        hid = keep.tile([P, PLACES, PACK], BF16, name="hid", align_bytes=64)
        for t in range(0, PACK, 2):
            nc.vector.tensor_tensor(
                hid[:, :, t : t + 2], met_a[:, t : t + 2, :].rearrange("p t o -> p o t"),
                met_b[:, t : t + 2, :].rearrange("p t o -> p o t"), MAX,
            )
        hq = keep.tile([P, PLACES], U32, name="hq", align_bytes=64)
        hs = keep.tile([P, PLACES], U8, name="hs", align_bytes=64)
        nc.vector.quantize_mx(out=hq[:].bitcast(FP8X4), scales=hs[:], in_=hid[:].rearrange("p o t -> p (o t)"))

        accs = []
        for h in range(2):
            cols = slice(P * h, P * (h + 1))
            acc = psum.tile([P, PLACES], F32, name=f"y_acc{h}", tag=f"bank{5 + h}")
            nc.tensor.matmul_mx(
                out=acc[:], lhsT=ws_w[:, cols].bitcast(FP8X4), lhsT_scale=ws_plane[:, cols],
                rhs=xr_gw[:].bitcast(FP4X4), rhs_scale=xr_gs[:], start=True, stop=False,
            )
            accs.append(acc)
        for h in range(2):
            cols = slice(P * h, P * (h + 1))
            nc.tensor.matmul_mx(
                out=accs[h][:], lhsT=wb_w[:, cols].bitcast(FP8X4), lhsT_scale=wb_plane[:, cols],
                rhs=hq[:].bitcast(FP8X4), rhs_scale=hs[:], start=False, stop=True,
            )
        y0 = keep.tile([P, PLACES], F32, name="y0")
        nc.scalar.copy(y0[:], accs[0][:])
        nc.scalar.dma_start(out[0:P, :], y0[:])
        y1 = keep.tile([P, PLACES], F32, name="y1")
        nc.vector.tensor_copy(y1[:], accs[1][:])
        nc.sync.dma_start(out[P : 2 * P, :], y1[:])
